import numpy as np
import ml_dtypes


def mxq(x, axis, fmt="e4m3"):
    dtype, down = {"e4m3": (ml_dtypes.float8_e4m3fn, 7), "e5m2": (ml_dtypes.float8_e5m2, 14)}[fmt]
    v = np.moveaxis(np.asarray(x, np.float32).astype(ml_dtypes.bfloat16).astype(np.float64), axis, -1)
    blocks = v.reshape(v.shape[:-1] + (-1, 32))
    amax = np.abs(blocks).max(-1, keepdims=True)
    byte = np.maximum(np.where(amax > 0, np.frexp(amax)[1] - 1 + 127, 0) - down, 1)
    scale = np.exp2(byte - 127.0)
    codes = (blocks / scale).astype(np.float32).astype(dtype).astype(np.float64)
    return np.moveaxis((codes * scale).reshape(v.shape), -1, axis)


WIDE = False


def mx_kscale(k):
    if not WIDE:
        return np.ones(k)
    levels = np.array([10, -10, 5, -5, 0])
    if k % 512:
        return np.exp2(np.random.permutation(np.resize(levels, k // 32))).repeat(32)
    a = np.empty((k // 512, 16))
    for p in range(k // 512):
        a[p, :8] = np.random.permutation(np.resize(levels, 8))
        for g in range(8):
            far = levels[np.abs(levels - a[p, g]) >= 10]
            a[p, g + 8] = far[np.random.randint(len(far))]
    return np.exp2(a.ravel()).repeat(32)


def f64(x):
    return np.asarray(x).astype(np.float64)


def striped(idx):
    return np.tile(idx.reshape(-1, 16).T, (8, 1)).astype(np.uint16)


def unstriped(offs):
    return offs[:16].T.reshape(-1).astype(np.int64)


E2M1 = np.array([0.0, 0.5, 1.0, 1.5, 2.0, 3.0, 4.0, 6.0, -0.0, -0.5, -1.0, -1.5, -2.0, -3.0, -4.0, -6.0])


def pack_weight(w, fmt):
    k, n = w.shape
    w = f64(np.asarray(w, np.float32).astype(ml_dtypes.bfloat16)).reshape(k // 32, 32, n)
    amax = np.abs(w).max(1)
    if fmt == "e4m3":
        byte = np.frexp(amax)[1] - 1 + 127 - 7
    else:
        mant, ex = np.frexp(amax / 6.0)
        byte = np.where(mant > 0.5, ex, ex - 1) + 127
    byte = np.clip(np.where(amax > 0, byte, 1), 1, 254)
    scaled = (w * np.exp2(127.0 - byte)[:, None, :]).reshape(k, n).astype(np.float32)
    by_word = np.ascontiguousarray(scaled.reshape(k // 512, 128, 4, n).transpose(0, 1, 3, 2))
    if fmt == "e4m3":
        words = by_word.astype(ml_dtypes.float8_e4m3fn).view(np.uint8)
    else:
        c = by_word.astype(ml_dtypes.float4_e2m1fn).view(np.uint8) & 0xF
        words = (c[..., 0::2] | (c[..., 1::2] << 4)).reshape(k // 512, 128, 2 * n)
    return np.ascontiguousarray(words), np.ascontiguousarray(byte.astype(np.uint8).reshape(k // 512, 16, n))


def unpack_weight(words, scales, fmt):
    g, _, n = scales.shape
    words = np.ascontiguousarray(words).reshape(g, 128, n, -1)
    if fmt == "e4m3":
        vals = words.view(ml_dtypes.float8_e4m3fn).astype(np.float64)
    else:
        nib = np.empty((g, 128, n, 4), np.uint8)
        nib[..., 0::2] = words & 0xF
        nib[..., 1::2] = words >> 4
        vals = E2M1[nib]
    vals = vals * np.repeat(np.exp2(scales.astype(np.float64) - 127.0), 8, axis=1)[..., None]
    return vals.transpose(0, 1, 3, 2).reshape(g * 512, n)


def gelu(v):
    return 0.5 * v * (1.0 + np.tanh(np.sqrt(2.0 / np.pi) * (v + 0.044715 * v**3)))


K, T, E, C, N = 1024, 1280, 8, 128, 128
K8 = 512


def by_expert(wq, xq):
    return np.concatenate([wq[e].T @ xq[:, e * C:(e + 1) * C] for e in range(E)], axis=1)


def setup_inputs():
    n = np.random.standard_normal
    s = mx_kscale(K)[:, None]
    w = n((E, K, N)) / np.sqrt(K) / s[None]
    w8 = [pack_weight(m[:K8], "e4m3") for m in w]
    w4 = [pack_weight(m[K8:], "e2m1") for m in w]
    return {
        "xT": (n((K, T)) * s).astype(np.float32),
        "xr": n((N, T)).astype(np.float32),
        "w8_words": np.stack([m[0] for m in w8]),
        "w8_scales": np.stack([m[1] for m in w8]),
        "w4_words": np.stack([m[0] for m in w4]),
        "w4_scales": np.stack([m[1] for m in w4]),
        "b": (0.3 * n((N, E))).astype(np.float32),
        "gate": np.tile(np.random.uniform(0.2, 1.0, E * C), (N, 1)).astype(np.float32),
        "offs": striped(np.random.permutation(T)[:E * C]),
    }


def reference(xT, xr, w8_words, w8_scales, w4_words, w4_scales, b, gate, offs):
    idx = unstriped(offs)
    w = np.stack([np.concatenate([unpack_weight(w8_words[e], w8_scales[e], "e4m3"), unpack_weight(w4_words[e], w4_scales[e], "e2m1")]) for e in range(E)])
    xq = mxq(f64(xT)[:, idx], 0, "e4m3")
    y = by_expert(w, xq)
    y = gelu(y + np.repeat(f64(b), C, axis=1))
    out = f64(xr).copy()
    out[:, idx] += f64(gate) * y
    return out

@@ -1,0 +1,151 @@
+from contextlib import ExitStack
+
+import concourse.mybir as mybir
+
+K, T, E, C, N = 1024, 1280, 8, 128, 128
+S = E * C
+FLOPS = 2 * S * K * N
+
+P = 128
+F32 = mybir.dt.float32
+BF16 = mybir.dt.bfloat16
+I32 = mybir.dt.int32
+U32 = mybir.dt.uint32
+U16 = mybir.dt.uint16
+U8 = mybir.dt.uint8
+FP8X4 = mybir.dt.float8_e4m3fn_x4
+FP4X4 = mybir.dt.float4_e2m1fn_x4
+COPY = mybir.ActivationFunctionType.Copy
+GELU = mybir.ActivationFunctionType.Gelu_apprx_tanh
+MULT = mybir.AluOpType.mult
+
+
+def tile_moe_res_lin_gelu_kernel(
+    tc, xT, xr, w8_words, w8_scales, w4_words, w4_scales, b, gate, offs, out
+):
+    nc = tc.nc
+    with ExitStack() as ctx:
+        held = ctx.enter_context(tc.tile_pool(name="held", bufs=1))
+        psum = ctx.enter_context(tc.psum_pool(name="psum", bufs=1))
+
+        offsets = held.tile([P, S // 16], U16, name="offsets")
+        codes = [held.tile([P, T], U32, name=f"codes{a}", align_bytes=64) for a in range(2)]
+        planes = held.tile([P, T], U8, name="planes", align_bytes=64)
+        slot_codes = [held.tile([P, S], U32, name=f"slot_codes{a}", align_bytes=64) for a in range(2)]
+        slot_planes = held.tile([P, S], U8, name="slot_planes", align_bytes=64)
+        w8 = held.tile([P, E * 512], U8, name="w8", align_bytes=64)
+        w4 = held.tile([P, E * 256], U8, name="w4", align_bytes=64)
+        w8_plane = held.tile([P, E * N], U8, name="w8_plane", align_bytes=64)
+        w4_plane = held.tile([P, E * N], U8, name="w4_plane", align_bytes=64)
+        bias = held.tile([P, E], F32, name="bias")
+        gates = held.tile([P, S], F32, name="gates")
+        resid = held.tile([P, T], F32, name="resid")
+        y = held.tile([P, S], F32, name="y")
+        gy = held.tile([P, S], F32, name="gy")
+        routed = held.tile([P, T], F32, name="routed")
+        total = held.tile([P, T], F32, name="total")
+        warm = held.tile([P, 8], F32, name="warm")
+        banks = [psum.tile([P, 512], F32, name=f"bank{e}") for e in range(E)]
+
+        nc.gpsimd.memset(warm[:], 0.0)
+        nc.gpsimd.memset(w8_plane[:].bitcast(I32), 0)
+        nc.gpsimd.memset(w4_plane[:].bitcast(I32), 0)
+        nc.gpsimd.memset(planes[:].bitcast(I32), 0)
+        nc.gpsimd.memset(routed[:], 0.0)
+        nc.scalar.activation(warm[:], warm[:], GELU)
+
+        x_view = xT.rearrange("(a p j) w -> a p j w", a=2, p=P, j=4)
+        chunks = (
+            (0, 0, 256, ((0, 256, False),)),
+            (0, 256, 768, ((256, 768, False),)),
+            (0, 768, 1280, ((768, 1024, False), (1024, 1280, True))),
+            (1, 0, 512, ((0, 512, False),)),
+            (1, 512, 1024, ((512, 768, False), (768, 1024, True))),
+            (1, 1024, 1280, ((1024, 1152, False), (1152, 1280, True))),
+        )
+        raw = []
+        for i, (a, lo, hi, units) in enumerate(chunks):
+            tile = held.tile([P, 4, hi - lo], F32, name=f"raw{i}")
+            nc.sync.dma_start(tile[:], x_view[a][:, :, lo:hi])
+            raw.append(tile)
+            if i == 0:
+                nc.sync.dma_start(offsets[:], offs)
+        w8_view = w8_words.rearrange("e a p n r -> p (e a) (n r)").bitcast(I32)
+        w4_view = w4_words.rearrange("e a p n -> p (e a) n").bitcast(I32)
+        w8_i = w8[:].bitcast(I32).rearrange("p (e n) -> p e n", e=E)
+        w4_i = w4[:].bitcast(I32).rearrange("p (e n) -> p e n", e=E)
+        for lo in range(0, E, 4):
+            nc.sync.dma_start(w8_i[:, lo : lo + 4, :], w8_view[:, lo : lo + 4, :])
+            nc.sync.dma_start(w4_i[:, lo : lo + 4, :], w4_view[:, lo : lo + 4, :])
+        nc.sync.dma_start(gates[:], gate)
+        nc.sync.dma_start(resid[:], xr)
+        for plane, scales in ((w8_plane, w8_scales), (w4_plane, w4_scales)):
+            src = scales.rearrange("e a q n -> q (e a) n").bitcast(I32)
+            dst = plane[:].bitcast(I32).rearrange("p (e n) -> p e n", e=E)
+            for quad in range(4):
+                nc.gpsimd.dma_start(dst[32 * quad : 32 * quad + 4], src[4 * quad : 4 * quad + 4])
+        nc.gpsimd.dma_start(bias[:], b)
+
+        def encode(src, a, lo, hi, vector):
+            name = f"grouped{a}_{lo}"
+            grouped = held.tile([P, hi - lo, 4], BF16, name=name, align_bytes=64)
+            dst = grouped[:].rearrange("p (w i) j -> p w j i", i=4)
+            src = src.rearrange("p j (w i) -> p w j i", i=4)
+            if vector:
+                nc.vector.tensor_copy(dst, src)
+            else:
+                nc.scalar.activation(dst, src, COPY)
+            first = 4 * (1 - a)
+            nc.vector.quantize_mx(
+                codes[a][:, lo:hi].bitcast(FP8X4), planes[first:P, lo:hi], grouped[:].rearrange("p w j -> p (w j)")
+            )
+
+        def gather(dst, src, lo, hi):
+            nc.vector.tensor_copy(dst[:, lo:hi], src[:].indirect(offsets[:, lo // 16 : hi // 16]))
+
+        def product(e, a):
+            slots = slice(e * C, (e + 1) * C)
+            if a == 0:
+                w = w8[:, 512 * e : 512 * (e + 1)].bitcast(FP8X4)
+                plane = w8_plane
+            else:
+                w = w4[:, 256 * e : 256 * (e + 1)].bitcast(FP4X4)
+                plane = w4_plane
+            nc.tensor.matmul_mx(
+                out=banks[e][:, :C],
+                lhsT=w,
+                lhsT_scale=plane[:, e * N : (e + 1) * N],
+                rhs=slot_codes[a][:, slots].bitcast(FP8X4),
+                rhs_scale=slot_planes[4 * (1 - a) : P, slots],
+                start=(a == 0),
+                stop=(a == 1),
+            )
+
+        for tile, (a, lo, hi, units) in zip(raw, chunks):
+            for u, v, vector in units:
+                encode(tile[:, :, u - lo : v - lo], a, u, v, vector)
+            if (a, hi) == (0, T):
+                for s in range(0, S, 512):
+                    gather(slot_codes[0], codes[0], s, s + 512)
+        for lo in range(0, S, 512):
+            gather(slot_planes, planes, lo, lo + 512)
+            for e in range(lo // C, (lo + 512) // C):
+                product(e, 0)
+            gather(slot_codes[1], codes[1], lo, lo + 512)
+            for e in range(lo // C, (lo + 512) // C):
+                product(e, 1)
+        Q = 256
+
+        def finish(i):
+            lo, hi = i * Q, (i + 1) * Q
+            for e in range(lo // C, hi // C):
+                nc.scalar.activation(y[:, e * C : (e + 1) * C], banks[e][:, :C], GELU, bias=bias[:, e : e + 1])
+            nc.gpsimd.tensor_tensor(gy[:, lo:hi], y[:, lo:hi], gates[:, lo:hi], MULT)
+            nc.vector.tensor_copy(routed[:].indirect(offsets[:, lo // 16 : hi // 16]), gy[:, lo:hi])
+        for i in range(S // Q):
+            finish(i)
+        for s in range(2):
+            cols = slice(s * T // 2, (s + 1) * T // 2)
+            nc.vector.tensor_add(total[:, cols], routed[:, cols], resid[:, cols])
+            queue = nc.sync if s == 0 else nc.scalar
+            queue.dma_start(out[:, cols], total[:, cols])

@@ -140,8 +140,7 @@ def tile_moe_res_lin_gelu_kernel(
             lo, hi = i * Q, (i + 1) * Q
             for e in range(lo // C, hi // C):
                 nc.scalar.activation(y[:, e * C : (e + 1) * C], banks[e][:, :C], GELU, bias=bias[:, e : e + 1])
-            nc.gpsimd.tensor_tensor(gy[:, lo:hi], y[:, lo:hi], gates[:, lo:hi], MULT)
-            nc.vector.tensor_copy(routed[:].indirect(offsets[:, lo // 16 : hi // 16]), gy[:, lo:hi])
+            nc.vector.tensor_tensor(routed[:].indirect(offsets[:, lo // 16 : hi // 16]), y[:, lo:hi], gates[:, lo:hi], MULT)
         for i in range(S // Q):
             finish(i)
         for s in range(2):

@@ -41,27 +41,25 @@ def tile_moe_res_lin_gelu_kernel(
         gates = held.tile([P, S], F32, name="gates")
         resid = held.tile([P, T], F32, name="resid")
         y = held.tile([P, S], F32, name="y")
-        gy = held.tile([P, S], F32, name="gy")
         routed = held.tile([P, T], F32, name="routed")
         total = held.tile([P, T], F32, name="total")
         warm = held.tile([P, 8], F32, name="warm")
         banks = [psum.tile([P, 512], F32, name=f"bank{e}") for e in range(E)]
 
         nc.gpsimd.memset(warm[:], 0.0)
+        nc.gpsimd.memset(planes[:].bitcast(I32), 0)
         nc.gpsimd.memset(w8_plane[:].bitcast(I32), 0)
         nc.gpsimd.memset(w4_plane[:].bitcast(I32), 0)
-        nc.gpsimd.memset(planes[:].bitcast(I32), 0)
         nc.gpsimd.memset(routed[:], 0.0)
         nc.scalar.activation(warm[:], warm[:], GELU)
 
         x_view = xT.rearrange("(a p j) w -> a p j w", a=2, p=P, j=4)
         chunks = (
-            (0, 0, 256, ((0, 256, False),)),
-            (0, 256, 768, ((256, 768, False),)),
-            (0, 768, 1280, ((768, 1024, False), (1024, 1280, True))),
+            (0, 0, 768, ((512, 768, True), (0, 512, False))),
+            (0, 768, 1280, ((1024, 1280, True), (768, 1024, False))),
             (1, 0, 512, ((0, 512, False),)),
-            (1, 512, 1024, ((512, 768, False), (768, 1024, True))),
-            (1, 1024, 1280, ((1024, 1152, False), (1152, 1280, True))),
+            (1, 512, 1024, ((768, 1024, True), (512, 768, False))),
+            (1, 1024, 1280, ((1152, 1280, True), (1024, 1152, False))),
         )
         raw = []
         for i, (a, lo, hi, units) in enumerate(chunks):
@@ -74,17 +72,24 @@ def tile_moe_res_lin_gelu_kernel(
         w4_view = w4_words.rearrange("e a p n -> p (e a) n").bitcast(I32)
         w8_i = w8[:].bitcast(I32).rearrange("p (e n) -> p e n", e=E)
         w4_i = w4[:].bitcast(I32).rearrange("p (e n) -> p e n", e=E)
-        for lo in range(0, E, 4):
-            nc.sync.dma_start(w8_i[:, lo : lo + 4, :], w8_view[:, lo : lo + 4, :])
-            nc.sync.dma_start(w4_i[:, lo : lo + 4, :], w4_view[:, lo : lo + 4, :])
-        nc.sync.dma_start(gates[:], gate)
-        nc.sync.dma_start(resid[:], xr)
-        for plane, scales in ((w8_plane, w8_scales), (w4_plane, w4_scales)):
+
+        def load_scales(plane, scales):
             src = scales.rearrange("e a q n -> q (e a) n").bitcast(I32)
             dst = plane[:].bitcast(I32).rearrange("p (e n) -> p e n", e=E)
             for quad in range(4):
-                nc.gpsimd.dma_start(dst[32 * quad : 32 * quad + 4], src[4 * quad : 4 * quad + 4])
-        nc.gpsimd.dma_start(bias[:], b)
+                nc.sync.dma_start(dst[32 * quad : 32 * quad + 4], src[4 * quad : 4 * quad + 4])
+
+        def load_words(lo, hi):
+            nc.sync.dma_start(w8_i[:, lo:hi, :], w8_view[:, lo:hi, :])
+            nc.sync.dma_start(w4_i[:, lo:hi, :], w4_view[:, lo:hi, :])
+
+        load_scales(w8_plane, w8_scales)
+        load_scales(w4_plane, w4_scales)
+        nc.sync.dma_start(bias[:], b)
+        load_words(0, 4)
+        nc.sync.dma_start(gates[:], gate)
+        load_words(4, 8)
+        nc.sync.dma_start(resid[:], xr)
 
         def encode(src, a, lo, hi, vector):
             name = f"grouped{a}_{lo}"
@@ -134,17 +139,11 @@ def tile_moe_res_lin_gelu_kernel(
             gather(slot_codes[1], codes[1], lo, lo + 512)
             for e in range(lo // C, (lo + 512) // C):
                 product(e, 1)
-        Q = 256
-
-        def finish(i):
-            lo, hi = i * Q, (i + 1) * Q
+        for lo in range(0, S, 512):
+            hi = lo + 512
             for e in range(lo // C, hi // C):
                 nc.scalar.activation(y[:, e * C : (e + 1) * C], banks[e][:, :C], GELU, bias=bias[:, e : e + 1])
             nc.vector.tensor_tensor(routed[:].indirect(offsets[:, lo // 16 : hi // 16]), y[:, lo:hi], gates[:, lo:hi], MULT)
-        for i in range(S // Q):
-            finish(i)
-        for s in range(2):
-            cols = slice(s * T // 2, (s + 1) * T // 2)
-            nc.vector.tensor_add(total[:, cols], routed[:, cols], resid[:, cols])
-            queue = nc.sync if s == 0 else nc.scalar
-            queue.dma_start(out[:, cols], total[:, cols])
+        for lo, hi, queue in ((0, 512, nc.sync), (512, 960, nc.scalar), (960, T, nc.sync)):
+            nc.vector.tensor_add(total[:, lo:hi], routed[:, lo:hi], resid[:, lo:hi])
+            queue.dma_start(out[:, lo:hi], total[:, lo:hi])

@@ -1,6 +1,7 @@
 from contextlib import ExitStack
 
 import concourse.mybir as mybir
+from concourse.masks import make_identity
 
 K, T, E, C, N = 1024, 1280, 8, 128, 128
 S = E * C
@@ -17,6 +18,7 @@ FP8X4 = mybir.dt.float8_e4m3fn_x4
 FP4X4 = mybir.dt.float4_e2m1fn_x4
 COPY = mybir.ActivationFunctionType.Copy
 GELU = mybir.ActivationFunctionType.Gelu_apprx_tanh
+ADD = mybir.AluOpType.add
 MULT = mybir.AluOpType.mult
 
 
@@ -44,34 +46,32 @@ def tile_moe_res_lin_gelu_kernel(
         routed = held.tile([P, T], F32, name="routed")
         total = held.tile([P, T], F32, name="total")
         warm = held.tile([P, 8], F32, name="warm")
-        banks = [psum.tile([P, 512], F32, name=f"bank{e}") for e in range(E)]
+        banks = [psum.tile([P, 512], F32, name=f"bank{e}") for e in range(4)]
+        NB = 4
 
         nc.gpsimd.memset(warm[:], 0.0)
         nc.gpsimd.memset(planes[:].bitcast(I32), 0)
         nc.gpsimd.memset(w8_plane[:].bitcast(I32), 0)
         nc.gpsimd.memset(w4_plane[:].bitcast(I32), 0)
         nc.gpsimd.memset(routed[:], 0.0)
+        ident = held.tile([P, P], F32, name="ident")
+        make_identity(nc, ident[:])
         nc.scalar.activation(warm[:], warm[:], GELU)
 
         x_view = xT.rearrange("(a p j) w -> a p j w", a=2, p=P, j=4)
-        chunks = (
-            (0, 0, 768, ((512, 768, True), (0, 512, False))),
-            (0, 768, 1280, ((1024, 1280, True), (768, 1024, False))),
-            (1, 0, 512, ((0, 512, False),)),
-            (1, 512, 1024, ((768, 1024, True), (512, 768, False))),
-            (1, 1024, 1280, ((1152, 1280, True), (1024, 1152, False))),
-        )
-        raw = []
-        for i, (a, lo, hi, units) in enumerate(chunks):
-            tile = held.tile([P, 4, hi - lo], F32, name=f"raw{i}")
-            nc.sync.dma_start(tile[:], x_view[a][:, :, lo:hi])
-            raw.append(tile)
-            if i == 0:
-                nc.sync.dma_start(offsets[:], offs)
         w8_view = w8_words.rearrange("e a p n r -> p (e a) (n r)").bitcast(I32)
         w4_view = w4_words.rearrange("e a p n -> p (e a) n").bitcast(I32)
         w8_i = w8[:].bitcast(I32).rearrange("p (e n) -> p e n", e=E)
         w4_i = w4[:].bitcast(I32).rearrange("p (e n) -> p e n", e=E)
+
+        chunks = ((0, 0, 4, 0, 768), (0, 0, 4, 768, T), (1, 0, 4, 0, 512), (1, 0, 4, 512, 1024), (1, 0, 4, 1024, T))
+        raw = []
+        for i, (a, j, k, lo, hi) in enumerate(chunks):
+            tile = held.tile([P, k - j, hi - lo], F32, name=f"raw{i}")
+            nc.sync.dma_start(tile[:], x_view[a][:, j:k, lo:hi])
+            raw.append(tile)
+            if i == 0:
+                nc.sync.dma_start(offsets[:], offs)
 
         def load_scales(plane, scales):
             src = scales.rearrange("e a q n -> q (e a) n").bitcast(I32)
@@ -91,18 +91,26 @@ def tile_moe_res_lin_gelu_kernel(
         load_words(4, 8)
         nc.sync.dma_start(resid[:], xr)
 
-        def encode(src, a, lo, hi, vector):
-            name = f"grouped{a}_{lo}"
-            grouped = held.tile([P, hi - lo, 4], BF16, name=name, align_bytes=64)
-            dst = grouped[:].rearrange("p (w i) j -> p w j i", i=4)
-            src = src.rearrange("p j (w i) -> p w j i", i=4)
+        def copy(dst, src, vector):
             if vector:
                 nc.vector.tensor_copy(dst, src)
             else:
                 nc.scalar.activation(dst, src, COPY)
+
+        def cast_half(grouped, src, h, vector):
+            copy(grouped[:, :, 2 * h : 2 * h + 2], src.rearrange("p j w -> p w j"), vector)
+
+        def cast(grouped, src, vector):
+            copy(
+                grouped[:].rearrange("p (w i) j -> p w j i", i=4), src.rearrange("p j (w i) -> p w j i", i=4), vector
+            )
+
+        def quantise(grouped, a, lo, hi, base):
             first = 4 * (1 - a)
             nc.vector.quantize_mx(
-                codes[a][:, lo:hi].bitcast(FP8X4), planes[first:P, lo:hi], grouped[:].rearrange("p w j -> p (w j)")
+                codes[a][:, lo:hi].bitcast(FP8X4),
+                planes[first:P, lo:hi],
+                grouped[:, lo - base : hi - base, :].rearrange("p w j -> p (w j)"),
             )
 
         def gather(dst, src, lo, hi):
@@ -117,7 +125,7 @@ def tile_moe_res_lin_gelu_kernel(
                 w = w4[:, 256 * e : 256 * (e + 1)].bitcast(FP4X4)
                 plane = w4_plane
             nc.tensor.matmul_mx(
-                out=banks[e][:, :C],
+                out=banks[e % NB][:, :C],
                 lhsT=w,
                 lhsT_scale=plane[:, e * N : (e + 1) * N],
                 rhs=slot_codes[a][:, slots].bitcast(FP8X4),
@@ -126,24 +134,48 @@ def tile_moe_res_lin_gelu_kernel(
                 stop=(a == 1),
             )
 
-        for tile, (a, lo, hi, units) in zip(raw, chunks):
-            for u, v, vector in units:
-                encode(tile[:, :, u - lo : v - lo], a, u, v, vector)
-            if (a, hi) == (0, T):
-                for s in range(0, S, 512):
-                    gather(slot_codes[0], codes[0], s, s + 512)
+        for i, (a, base, units) in enumerate((
+            (0, 0, ((512, 768, True), (0, 512, False))),
+            (0, 768, ((1024, 1280, True), (768, 1024, False))),
+            (1, 0, ((0, 512, False),)),
+            (1, 512, ((768, 1024, True), (512, 768, False))),
+            (1, 1024, ((1152, 1280, True), (1024, 1152, False))),
+        )):
+            for lo, hi, vector in units:
+                grouped = held.tile([P, hi - lo, 4], BF16, name=f"grouped{a}_{lo}", align_bytes=64)
+                cast(grouped, raw[i][:, :, lo - base : hi - base], vector)
+                quantise(grouped, a, lo, hi, lo)
+            if i == 1:
+                for lo in range(0, S, 512):
+                    gather(slot_codes[0], codes[0], lo, lo + 512)
+
         for lo in range(0, S, 512):
             gather(slot_planes, planes, lo, lo + 512)
-            for e in range(lo // C, (lo + 512) // C):
-                product(e, 0)
             gather(slot_codes[1], codes[1], lo, lo + 512)
             for e in range(lo // C, (lo + 512) // C):
+                product(e, 0)
+            for e in range(lo // C, (lo + 512) // C):
                 product(e, 1)
+                nc.scalar.activation(y[:, e * C : (e + 1) * C], banks[e % NB][:, :C], GELU, bias=bias[:, e : e + 1])
+        V = 960
+        VT = 1024
+        flips = [psum.tile([P, 512], F32, name=f"flip{i}") for i in range(2)]
+        backs = [psum.tile([P, 512], F32, name=f"back{i}") for i in range(2)]
+        flipped = held.tile([P, VT], F32, name="flipped")
+        for i, lo in enumerate(range(0, VT, 512)):
+            hi = lo + 512
+            for c in range(lo, hi, P):
+                nc.tensor.transpose(flips[i][:, c - lo : c - lo + P], resid[:, c : c + P], ident[:])
+            nc.scalar.copy(flipped[:, lo:hi], flips[i][:, : hi - lo])
+        for i, lo in enumerate(range(0, VT, 512)):
+            for c in range(lo, lo + 512, P):
+                nc.tensor.transpose(backs[i][:, c - lo : c - lo + P], flipped[:, c : c + P], ident[:])
         for lo in range(0, S, 512):
             hi = lo + 512
-            for e in range(lo // C, hi // C):
-                nc.scalar.activation(y[:, e * C : (e + 1) * C], banks[e][:, :C], GELU, bias=bias[:, e : e + 1])
             nc.vector.tensor_tensor(routed[:].indirect(offsets[:, lo // 16 : hi // 16]), y[:, lo:hi], gates[:, lo:hi], MULT)
-        for lo, hi, queue in ((0, 512, nc.sync), (512, 960, nc.scalar), (960, T, nc.sync)):
-            nc.vector.tensor_add(total[:, lo:hi], routed[:, lo:hi], resid[:, lo:hi])
-            queue.dma_start(out[:, lo:hi], total[:, lo:hi])
+        nc.gpsimd.tensor_tensor(total[:, V:T], routed[:, V:T], resid[:, V:T], ADD)
+        nc.sync.dma_start(out[:, V:T], total[:, V:T])
+        for i, lo in enumerate(range(0, V, 512)):
+            hi = min(lo + 512, V)
+            nc.vector.tensor_tensor(total[:, lo:hi], backs[i][:, : hi - lo], routed[:, lo:hi], ADD)
+            nc.sync.dma_start(out[:, lo:hi], total[:, lo:hi])

from contextlib import ExitStack

import concourse.mybir as mybir
from concourse.masks import make_identity

K, T, E, C, N = 1024, 1280, 8, 128, 128
S = E * C
FLOPS = 2 * S * K * N

P = 128
F32 = mybir.dt.float32
BF16 = mybir.dt.bfloat16
I32 = mybir.dt.int32
U32 = mybir.dt.uint32
U16 = mybir.dt.uint16
U8 = mybir.dt.uint8
FP8X4 = mybir.dt.float8_e4m3fn_x4
FP4X4 = mybir.dt.float4_e2m1fn_x4
COPY = mybir.ActivationFunctionType.Copy
GELU = mybir.ActivationFunctionType.Gelu_apprx_tanh
ADD = mybir.AluOpType.add
MULT = mybir.AluOpType.mult


def tile_moe_res_lin_gelu_kernel(
    tc, xT, xr, w8_words, w8_scales, w4_words, w4_scales, b, gate, offs, out
):
    nc = tc.nc
    with ExitStack() as ctx:
        held = ctx.enter_context(tc.tile_pool(name="held", bufs=1))
        psum = ctx.enter_context(tc.psum_pool(name="psum", bufs=1))

        offsets = held.tile([P, S // 16], U16, name="offsets")
        codes = [held.tile([P, T], U32, name=f"codes{a}", align_bytes=64) for a in range(2)]
        planes = held.tile([P, T], U8, name="planes", align_bytes=64)
        slot_codes = [held.tile([P, S], U32, name=f"slot_codes{a}", align_bytes=64) for a in range(2)]
        slot_planes = held.tile([P, S], U8, name="slot_planes", align_bytes=64)
        w8 = held.tile([P, E * 512], U8, name="w8", align_bytes=64)
        w4 = held.tile([P, E * 256], U8, name="w4", align_bytes=64)
        w8_plane = held.tile([P, E * N], U8, name="w8_plane", align_bytes=64)
        w4_plane = held.tile([P, E * N], U8, name="w4_plane", align_bytes=64)
        bias = held.tile([P, E], F32, name="bias")
        gates = held.tile([P, S], F32, name="gates")
        resid = held.tile([P, T], F32, name="resid")
        y = held.tile([P, S], F32, name="y")
        routed = held.tile([P, T], F32, name="routed")
        total = held.tile([P, T], F32, name="total")
        warm = held.tile([P, 8], F32, name="warm")
        banks = [psum.tile([P, 512], F32, name=f"bank{e}") for e in range(4)]
        NB = 4

        nc.gpsimd.memset(warm[:], 0.0)
        nc.gpsimd.memset(planes[:].bitcast(I32), 0)
        nc.gpsimd.memset(w8_plane[:].bitcast(I32), 0)
        nc.gpsimd.memset(w4_plane[:].bitcast(I32), 0)
        nc.gpsimd.memset(routed[:], 0.0)
        ident = held.tile([P, P], F32, name="ident")
        make_identity(nc, ident[:])
        nc.scalar.activation(warm[:], warm[:], GELU)

        x_view = xT.rearrange("(a p j) w -> a p j w", a=2, p=P, j=4)
        w8_view = w8_words.rearrange("e a p n r -> p (e a) (n r)").bitcast(I32)
        w4_view = w4_words.rearrange("e a p n -> p (e a) n").bitcast(I32)
        w8_i = w8[:].bitcast(I32).rearrange("p (e n) -> p e n", e=E)
        w4_i = w4[:].bitcast(I32).rearrange("p (e n) -> p e n", e=E)

        chunks = ((0, 0, 4, 0, 768), (0, 0, 4, 768, T), (1, 0, 4, 0, 512), (1, 0, 4, 512, 1024), (1, 0, 4, 1024, T))
        raw = []
        for i, (a, j, k, lo, hi) in enumerate(chunks):
            tile = held.tile([P, k - j, hi - lo], F32, name=f"raw{i}")
            nc.sync.dma_start(tile[:], x_view[a][:, j:k, lo:hi])
            raw.append(tile)
            if i == 0:
                nc.sync.dma_start(offsets[:], offs)

        def load_scales(plane, scales):
            src = scales.rearrange("e a q n -> q (e a) n").bitcast(I32)
            dst = plane[:].bitcast(I32).rearrange("p (e n) -> p e n", e=E)
            for quad in range(4):
                nc.sync.dma_start(dst[32 * quad : 32 * quad + 4], src[4 * quad : 4 * quad + 4])

        def load_words(lo, hi):
            nc.sync.dma_start(w8_i[:, lo:hi, :], w8_view[:, lo:hi, :])
            nc.sync.dma_start(w4_i[:, lo:hi, :], w4_view[:, lo:hi, :])

        load_scales(w8_plane, w8_scales)
        load_scales(w4_plane, w4_scales)
        nc.sync.dma_start(bias[:], b)
        load_words(0, 4)
        nc.sync.dma_start(gates[:], gate)
        load_words(4, 8)
        nc.sync.dma_start(resid[:], xr)

        def copy(dst, src, vector):
            if vector:
                nc.vector.tensor_copy(dst, src)
            else:
                nc.scalar.activation(dst, src, COPY)

        def cast_half(grouped, src, h, vector):
            copy(grouped[:, :, 2 * h : 2 * h + 2], src.rearrange("p j w -> p w j"), vector)

        def cast(grouped, src, vector):
            copy(
                grouped[:].rearrange("p (w i) j -> p w j i", i=4), src.rearrange("p j (w i) -> p w j i", i=4), vector
            )

        def quantise(grouped, a, lo, hi, base):
            first = 4 * (1 - a)
            nc.vector.quantize_mx(
                codes[a][:, lo:hi].bitcast(FP8X4),
                planes[first:P, lo:hi],
                grouped[:, lo - base : hi - base, :].rearrange("p w j -> p (w j)"),
            )

        def gather(dst, src, lo, hi):
            nc.vector.tensor_copy(dst[:, lo:hi], src[:].indirect(offsets[:, lo // 16 : hi // 16]))

        def product(e, a):
            slots = slice(e * C, (e + 1) * C)
            if a == 0:
                w = w8[:, 512 * e : 512 * (e + 1)].bitcast(FP8X4)
                plane = w8_plane
            else:
                w = w4[:, 256 * e : 256 * (e + 1)].bitcast(FP4X4)
                plane = w4_plane
            nc.tensor.matmul_mx(
                out=banks[e % NB][:, :C],
                lhsT=w,
                lhsT_scale=plane[:, e * N : (e + 1) * N],
                rhs=slot_codes[a][:, slots].bitcast(FP8X4),
                rhs_scale=slot_planes[4 * (1 - a) : P, slots],
                start=(a == 0),
                stop=(a == 1),
            )

        for i, (a, base, units) in enumerate((
            (0, 0, ((512, 768, True), (0, 512, False))),
            (0, 768, ((1024, 1280, True), (768, 1024, False))),
            (1, 0, ((0, 512, False),)),
            (1, 512, ((768, 1024, True), (512, 768, False))),
            (1, 1024, ((1152, 1280, True), (1024, 1152, False))),
        )):
            for lo, hi, vector in units:
                grouped = held.tile([P, hi - lo, 4], BF16, name=f"grouped{a}_{lo}", align_bytes=64)
                cast(grouped, raw[i][:, :, lo - base : hi - base], vector)
                quantise(grouped, a, lo, hi, lo)
            if i == 1:
                for lo in range(0, S, 512):
                    gather(slot_codes[0], codes[0], lo, lo + 512)

        for lo in range(0, S, 512):
            gather(slot_planes, planes, lo, lo + 512)
            gather(slot_codes[1], codes[1], lo, lo + 512)
            for e in range(lo // C, (lo + 512) // C):
                product(e, 0)
            for e in range(lo // C, (lo + 512) // C):
                product(e, 1)
                nc.scalar.activation(y[:, e * C : (e + 1) * C], banks[e % NB][:, :C], GELU, bias=bias[:, e : e + 1])
        V = 960
        VT = 1024
        flips = [psum.tile([P, 512], F32, name=f"flip{i}") for i in range(2)]
        backs = [psum.tile([P, 512], F32, name=f"back{i}") for i in range(2)]
        flipped = held.tile([P, VT], F32, name="flipped")
        for i, lo in enumerate(range(0, VT, 512)):
            hi = lo + 512
            for c in range(lo, hi, P):
                nc.tensor.transpose(flips[i][:, c - lo : c - lo + P], resid[:, c : c + P], ident[:])
            nc.scalar.copy(flipped[:, lo:hi], flips[i][:, : hi - lo])
        for i, lo in enumerate(range(0, VT, 512)):
            for c in range(lo, lo + 512, P):
                nc.tensor.transpose(backs[i][:, c - lo : c - lo + P], flipped[:, c : c + P], ident[:])
        for lo in range(0, S, 512):
            hi = lo + 512
            nc.vector.tensor_tensor(routed[:].indirect(offsets[:, lo // 16 : hi // 16]), y[:, lo:hi], gates[:, lo:hi], MULT)
        nc.gpsimd.tensor_tensor(total[:, V:T], routed[:, V:T], resid[:, V:T], ADD)
        nc.sync.dma_start(out[:, V:T], total[:, V:T])
        for i, lo in enumerate(range(0, V, 512)):
            hi = min(lo + 512, V)
            nc.vector.tensor_tensor(total[:, lo:hi], backs[i][:, : hi - lo], routed[:, lo:hi], ADD)
            nc.sync.dma_start(out[:, lo:hi], total[:, lo:hi])
